import numpy as np
CORES = [5,13,29,37,53,69,77,101,133,141,157,165,181,197,205,229]
N = 16
T, CAP = 256, 96
def entries(a): return a.T.reshape(-1)
def pack(v, P): return np.ascontiguousarray(np.asarray(v, np.int32).reshape(-1, P).T)
def lists(rng, how):
    n = rng.integers(1, CAP + 1, N)
    if how == "none": n[rng.integers(N)] = 0; n[rng.integers(N)] = 0
    if how == "full": n[:] = CAP
    if how == "one": n[:] = 1
    if how == "void": n[:] = 0
    Kp = np.zeros((N, T), np.int32)
    for r in range(N): Kp[r, (np.arange(T - n[r], T) if how == "last" else rng.permutation(T)[:n[r]])] = 1
    return {"keep": np.stack([pack(Kp[r], 16) for r in range(N)])}
def setup_inputs(rng):
    return dict({"x": rng.standard_normal((N, 128, T), dtype=np.float32)}, **lists(rng, "uniform"))
def setup_inputs_full(rng):
    d = setup_inputs(rng); d.update(lists(rng, "full"))
    for k in ("x",): d[k] = (d[k].astype(np.float32) * 1048576.0).astype(d[k].dtype)
    return d
def setup_inputs_last(rng):
    d = setup_inputs(rng); d.update(lists(rng, "last"))
    for k in ("x",): d[k] = (d[k].astype(np.float32) * (1 / 1024.0)).astype(d[k].dtype)
    return d
def setup_inputs_none(rng):
    d = setup_inputs(rng); d.update(lists(rng, "none"))
    return d
def setup_inputs_one(rng):
    d = setup_inputs(rng); d.update(lists(rng, "one"))
    return d
def setup_inputs_void(rng):
    d = setup_inputs(rng); d.update(lists(rng, "void"))
    return d
def check_inputs(x):
    bad = []
    if x["keep"].min() < 0 or x["keep"].max() >= 2: bad.append("keep out of range")
    if max(int(a.sum()) for a in x["keep"]) > CAP: bad.append("a rank keeps more than CAP")
    return bad
def reference(x, keep):
    kept = np.concatenate([x[r][:, entries(keep[r]) == 1] for r in range(N)], axis=1)
    y = np.zeros((128, N * CAP), x.dtype); y[:, :kept.shape[1]] = kept
    return {"y": np.broadcast_to(y, (N, 128, N * CAP))}

@@ -1,0 +1,250 @@
+from concourse.bass import DstId, RemoteDMATransfer
+from concourse.mybir import AluOpType, AxisListType, ActivationFunctionType
+
+NSIM = 256
+N, TC, CAP = 16, 256, 96
+W = N * CAP
+CAPS = (3, 3, 2, 2, 1, 1)
+VCH = ((0, 24), (24, 48))
+ACH = ((48, 72), (72, 96))
+
+SCRATCH = {
+    "xin": ("sbuf", [128, TC], "float32"),
+    "xs": ("sbuf", [128, TC], "float32"),
+    "hb": ("sbuf", [128, CAP], "float32"),
+    "land": ("sbuf", [128, W + 4], "float32"),
+    "yo": ("sbuf", [128, W], "float32"),
+    "kd": ("dram", [128, 2], "int32"),
+    "kall": ("dram", [N, 128, 2], "int32"),
+    "kp": ("sbuf", [128, 16], "int32"),
+    "kk": ("sbuf", [128, TC], "int32"),
+    "kkf": ("sbuf", [128, TC], "float32"),
+    "mmod": ("sbuf", [128, 128], "float32"),
+    "kidx": ("sbuf", [128, 1], "float32"),
+    "nck": ("sbuf", [128, 16], "int32"),
+    "c16x": ("sbuf", [128, 97], "float32"),
+    "ones": ("sbuf", [128, 128], "bfloat16"),
+    "zer": ("sbuf", [128, 16], "bfloat16"),
+    "rm": ("sbuf", [128, 128], "bfloat16"),
+    "wp": ("sbuf", [128, 128], "bfloat16"),
+    "ck": ("sbuf", [128, 16], "bfloat16"),
+    "cq1": ("sbuf", [128, 96], "bfloat16"),
+    "cq2": ("sbuf", [128, 96], "bfloat16"),
+    "tri": ("sbuf", [128, 16], "bfloat16"),
+    "kpf": ("sbuf", [128, 16], "bfloat16"),
+    "kneg": ("sbuf", [128, 16], "bfloat16"),
+    "xinc": ("sbuf", [128, 16], "bfloat16"),
+    "dst16": ("sbuf", [128, 16], "uint16"),
+    "nf": ("sbuf", [128, 1], "float32"),
+    "nb": ("sbuf", [128, 1], "bfloat16"),
+    "gap": ("sbuf", [128, 1], "float32"),
+    "offp": ("sbuf", [128, 1], "float32"),
+    "offi": ("sbuf", [128, 1], "int32"),
+    "loi": ("sbuf", [128, 1], "int32"),
+    "lo": ("sbuf", [128, 1], "float32"),
+    "rhx": ("sbuf", [128, 97], "bfloat16"),
+    "lta": ("sbuf", [128, 128], "bfloat16"),
+    "ltb": ("sbuf", [128, 128], "bfloat16"),
+    "offs": ("sbuf", [128, 96], "uint16"),
+    "psd": ("psum", [128, 512], "float32"),
+    "psf": ("psum", [128, 512], "float32"),
+    "pso": ("psum", [128, 512], "float32"),
+}
+SEMAPHORES = ["c0", "cv", "kld", "xld", "kown", "karr", "kload", "a1", "a2", "a3", "a4", "bready", "own", "arrived",
+              "b1", "b2", "b3", "b4", "b5", "b6", "b7", "b8", "b9", "b10", "b11", "st", "sent",
+              "g0", "g1", "g2", "g3", "g4", "g5", "g6", "g7"]
+
+
+def make_plan(cores, topo):
+    load = {}
+    plan = []
+    for s, R in enumerate(cores):
+        mates = [c for c in range(NSIM) if c != R and topo.host(c) == topo.host(R) and topo.chip(c) == topo.chip(R)]
+        others = [cores[(s + 1 + j) % len(cores)] for j in range(len(cores) - 1)]
+        cross = [d for d in others if not topo.may_write(R, d)]
+        same = [d for d in others if topo.may_write(R, d)]
+        owners = [c for c in mates if all(topo.may_write(c, d) for d in others)]
+        plain = [c for c in mates if c not in owners]
+        near, far = topo.die(R), 1 - topo.die(R)
+        H = ([c for c in owners if topo.die(c) == far][:2] + [c for c in owners if topo.die(c) == near][:2]
+             + [c for c in plain if topo.die(c) == far][:2])
+        cap = dict(zip(H, CAPS))
+        cap[R] = len(others) - sum(CAPS)
+        far_own = sum(cap[c] for c in H[0:2])
+        near_own = sum(cap[c] for c in H[2:4])
+        far_all = far_own + sum(cap[c] for c in H[4:6])
+        fc = min(far_own, max(len(cross) - near_own, (len(cross) + 1) // 2))
+
+        def lean(d):
+            return load.get((d, far), 0) - load.get((d, near), 0)
+        cs = sorted(cross, key=lean)
+        ss = sorted(same, key=lean)
+        cf, cn = cs[:fc], cs[fc:]
+        sf, sn = ss[:far_all - fc], ss[far_all - fc:]
+        give = dict((c, []) for c in H + [R])
+
+        def deal(ds, cs_):
+            for d in ds:
+                c = [c for c in cs_ if len(give[c]) < cap[c]][0]
+                give[c].append(d)
+                load[(d, topo.die(c))] = load.get((d, topo.die(c)), 0) + 1
+        deal(cf, H[0:2])
+        deal(cn, H[2:4])
+        deal(sf, H[4:6] + H[0:2])
+        deal(sn, [R] + H[2:4])
+        plan.append({"R": R, "H": H, "give": give})
+    return plan
+
+
+def _send(g, T, topo, core, groups, src, dst_of, rsem):
+    trs = []
+    for m, ds in groups:
+        ids = []
+        for d in ds:
+            rid, pid = topo.addr(d, core)
+            ids.append(DstId(rid=rid, pnc=pid))
+        trs.append(RemoteDMATransfer(dst_ids=ids, dma_engine_mask=m, remote_sem=rsem, srcs=[src],
+                                     dsts=[dst_of(d) for d in ds]))
+    g.remote_dma_fused(trs, local_sem=T.sem.sent)
+    return sum(bin(m).count("1") for m, ds in groups)
+
+
+def rank_program(g, core, T, topo):
+    plan = make_plan(list(T.cores), topo)
+    rank = T.rank_of(core)
+    if rank is None:
+        for s, p in enumerate(plan):
+            if core in p["H"] and p["give"][core]:
+                helper_program(g, core, T, topo, s, p)
+        return
+    s, p = rank, plan[rank]
+    V, PE, ACT, SY = g.vector, g.tensor, g.scalar, g.sync
+    S = T.sem
+    A = AluOpType
+    P16 = slice(0, 16)
+
+    ACT.dma_start(T.kp[P16, 0:16], T.keep[:]).then_inc(S.kld, 16)
+    SY.dma_start(T.xin[:, :], T.x[:]).then_inc(S.xld, 16)
+    ACT.dma_start(T.kall[s], T.keep[:]).then_inc(S.kown, 16)
+
+    g.iota(T.mmod[P16, :], [[0, 8], [1, 16]], 0, 0, allow_small_or_imprecise_dtypes=True).then_inc(S.c0, 1)
+    g.iota(T.kidx[P16, :], [[0, 1]], 0, 1, allow_small_or_imprecise_dtypes=True).then_inc(S.c0, 1)
+    g.iota(T.nck[P16, :], [[16, 16]], -255, 1).then_inc(S.c0, 1)
+    g.iota(T.c16x[P16, :], [[16, 97]], 0, 0, allow_small_or_imprecise_dtypes=True).then_inc(S.c0, 1)
+    V.memset(T.ones[P16, :], 1.0).then_inc(S.cv, 1)
+    V.memset(T.zer[P16, :], 0.0).then_inc(S.cv, 1)
+    V.memset(T.land[:, W:W + 4], 0.0).then_inc(S.cv, 1)
+    V.wait_ge(S.c0, 4)
+    kx = T.kidx[P16, 0:1]
+    V.tensor_scalar(T.rm[P16, :], T.mmod[P16, :], kx, None, A.is_equal).then_inc(S.cv, 1)
+    V.tensor_scalar(T.wp[P16, :], T.mmod[P16, :], kx, -1.0, A.is_le, A.mult).then_inc(S.cv, 1)
+    V.tensor_scalar(T.ck[P16, :], T.nck[P16, :], -1.0, None, A.mult).then_inc(S.cv, 1)
+    V.tensor_scalar(T.cq1[P16, :], T.c16x[P16, 0:96], 0.0, kx, A.mult, A.add).then_inc(S.cv, 1)
+    V.tensor_copy(T.cq2[P16, :], T.c16x[P16, 0:96]).then_inc(S.cv, 1)
+    V.tensor_scalar(T.tri[P16, :], T.mmod[P16, 0:16], kx, None, A.is_ge).then_inc(S.cv, 1)
+    NCV = 9
+    V.wait_ge(S.cv, NCV)
+    PE.wait_ge(S.cv, NCV)
+    PE.matmul(T.psd[:, 0:16], T.rm[P16, :], T.ck[P16, :], True, False).then_inc(S.a3, 1)
+    PE.matmul(T.psf[:, 0:96], T.rm[P16, :], T.cq1[P16, :], True, False).then_inc(S.b9, 1)
+    PE.matmul(T.psf[:, 0:96], T.rm[P16, :], T.cq2[P16, :], False, False).then_inc(S.b9, 1)
+
+    V.wait_ge(S.kld, 16)
+    V.tensor_copy(T.kpf[P16, :], T.kp[P16, :]).then_inc(S.a1, 1)
+    V.tensor_tensor(T.kneg[P16, :], T.kp[P16, :], T.nck[P16, :], A.mult).then_inc(S.a1, 1)
+    V.wait_ge(S.a1, 2)
+    V.tensor_tensor_scan(T.xinc[P16, :], T.kpf[P16, :], T.zer[P16, :], 0.0, A.add, A.add).then_inc(S.a2, 1)
+    PE.wait_ge(S.a1, 2)
+    PE.matmul(T.psd[:, 0:16], T.wp[P16, :], T.kpf[P16, :], False, False).then_inc(S.a3, 1)
+    PE.matmul(T.psd[:, 0:16], T.rm[P16, :], T.kneg[P16, :], False, False).then_inc(S.a3, 1)
+    PE.wait_ge(S.a2, 1)
+    PE.matmul(T.psd[:, 0:16], T.ones[P16, :], T.xinc[P16, :], False, True).then_inc(S.a3, 1)
+    V.wait_ge(S.a3, 4)
+    V.tensor_copy(T.dst16[:, :], T.psd[:, 0:16]).then_inc(S.a4, 1)
+    V.wait_ge(S.a4, 1)
+    V.wait_ge(S.xld, 16)
+    V.tensor_copy(T.xs[:, 0:TC].indirect(T.dst16[:, 0:16]), T.xin[:, :]).then_inc(S.bready, 1)
+
+    H, give = p["H"], p["give"]
+    lo_m = topo.mask(core, give[core][0])
+    hi_m = topo.mask(core, H[0]) & ~lo_m
+    groups = [(hi_m, H[0::2]), (lo_m, H[1::2] + give[core])]
+    g.wait_ge(S.kown, 16)
+    sent = _send(g, T, topo, core, groups, T.kall[s], lambda d: T.kd[:] if d in H else T.kall[s], S.karr)
+    g.wait_ge(S.bready, 1)
+    slot = T.land[:, CAP * s:CAP * (s + 1)]
+    sent += _send(g, T, topo, core, groups, T.xs[:, 0:CAP], lambda d: T.hb[:, :] if d in H else slot, S.arrived)
+
+    V.wait_ge(S.bready, 1)
+    V.tensor_copy(slot, T.xs[:, 0:CAP]).then_inc(S.own, 1)
+
+    ne = bin(lo_m).count("1")
+    SY.wait_ge(S.kown, 16)
+    SY.wait_ge(S.karr, ne * (N - 1))
+    SY.dma_start(T.kk[P16, :], T.kall[:]).then_inc(S.kload, 16)
+    V.wait_ge(S.kload, 16)
+    V.tensor_copy(T.kkf[P16, :], T.kk[P16, :]).then_inc(S.b1, 1)
+    V.wait_ge(S.b1, 1)
+    V.tensor_reduce(T.nf[P16, :], T.kkf[P16, :], AxisListType.X, A.add).then_inc(S.b2, 1)
+    V.wait_ge(S.b2, 1)
+    V.tensor_copy(T.nb[P16, :], T.nf[P16, :]).then_inc(S.b3, 1)
+    V.tensor_scalar(T.gap[P16, :], T.nf[P16, :], -1.0, float(CAP), A.mult, A.add).then_inc(S.b3, 1)
+    PE.wait_ge(S.b3, 2)
+    PE.matmul(T.pso[P16, 0:1], T.tri[P16, :], T.nb[P16, :], True, True).then_inc(S.b4, 1)
+    V.wait_ge(S.b3, 2)
+    V.wait_ge(S.b4, 1)
+    V.tensor_copy(T.offp[P16, :], T.pso[P16, 0:1]).then_inc(S.b5, 1)
+    V.tensor_copy(T.offi[P16, :], T.pso[P16, 0:1]).then_inc(S.b5, 1)
+    V.wait_ge(S.b5, 2)
+    V.tensor_scalar(T.rhx[P16, :], T.c16x[P16, :], T.offp[P16, 0:1], None, A.is_gt).then_inc(S.b6, 1)
+    V.tensor_scalar(T.loi[P16, :], T.offi[P16, :], 15, None, A.bitwise_and).then_inc(S.b7, 1)
+    V.wait_ge(S.b7, 1)
+    V.tensor_copy(T.lo[P16, :], T.loi[P16, :]).then_inc(S.b8, 1)
+    V.wait_ge(S.b8, 1)
+    V.tensor_scalar(T.lta[P16, :], T.mmod[P16, :], T.lo[P16, 0:1], T.gap[P16, 0:1], A.is_lt, A.mult).then_inc(S.b6, 1)
+    V.tensor_scalar(T.ltb[P16, :], T.mmod[P16, :], T.lo[P16, 0:1], T.gap[P16, 0:1], A.is_ge, A.mult).then_inc(S.b6, 1)
+    PE.wait_ge(S.b6, 3)
+    PE.matmul(T.psf[:, 0:96], T.lta[P16, :], T.rhx[P16, 0:96], False, False).then_inc(S.b9, 1)
+    PE.matmul(T.psf[:, 0:96], T.ltb[P16, :], T.rhx[P16, 1:97], False, True).then_inc(S.b9, 1)
+    V.wait_ge(S.b6, 3)
+    V.wait_ge(S.b9, 4)
+    V.tensor_scalar(T.offs[:, :], T.psf[:, 0:96], float(W), None, A.min).then_inc(S.b10, 1)
+
+    win = T.land[:, 0:W + 1]
+    for q in (V, ACT):
+        q.wait_ge(S.b10, 1)
+        q.wait_ge(S.own, 1)
+        q.wait_ge(S.arrived, ne * (N - 1))
+    order = []
+    for j in range(max(len(VCH), len(ACH))):
+        if j < len(VCH):
+            a, b = VCH[j]
+            sem = S["g%d" % (2 * j)]
+            V.tensor_copy(T.yo[:, 16 * a:16 * b], win.indirect(T.offs[:, a:b])).then_inc(sem, 1)
+            order.append((sem, a, b))
+        if j < len(ACH):
+            a, b = ACH[j]
+            sem = S["g%d" % (2 * j + 1)]
+            ACT.activation(T.yo[:, 16 * a:16 * b], win.indirect(T.offs[:, a:b]), ActivationFunctionType.Identity,
+                           bias=-0.0).then_inc(sem, 1)
+            order.append((sem, a, b))
+    for sem, a, b in order:
+        SY.wait_ge(sem, 1)
+        SY.dma_start(T.y[:, 16 * a:16 * b], T.yo[:, 16 * a:16 * b]).then_inc(S.st, 16)
+    SY.wait_ge(S.st, 16 * len(order))
+    g.wait_ge(S.sent, sent)
+
+
+def helper_program(g, core, T, topo, s, p):
+    S = T.sem
+    ds = p["give"][core]
+    m = topo.mask(core, ds[0])
+    R = p["R"]
+    lo_m = topo.mask(R, p["give"][R][0])
+    hi_m = topo.mask(R, core) & ~lo_m
+    got = bin(hi_m if p["H"].index(core) % 2 == 0 else lo_m).count("1")
+    g.wait_ge(S.karr, got)
+    sent = _send(g, T, topo, core, [(m, ds)], T.kd[:], lambda d: T.kall[s], S.karr)
+    g.wait_ge(S.arrived, got)
+    sent += _send(g, T, topo, core, [(m, ds)], T.hb[:, :], lambda d: T.land[:, CAP * s:CAP * (s + 1)], S.arrived)
+    g.wait_ge(S.sent, sent)

@@ -4,9 +4,11 @@ from concourse.mybir import AluOpType, AxisListType, ActivationFunctionType
 NSIM = 256
 N, TC, CAP = 16, 256, 96
 W = N * CAP
-CAPS = (3, 3, 2, 2, 1, 1)
+CAPS = (4, 3, 3, 2, 2, 1)
 VCH = ((0, 24), (24, 48))
 ACH = ((48, 72), (72, 96))
+KP = 64
+KW = N * TC // KP
 
 SCRATCH = {
     "xin": ("sbuf", [128, TC], "float32"),
@@ -17,26 +19,27 @@ SCRATCH = {
     "kd": ("dram", [128, 2], "int32"),
     "kall": ("dram", [N, 128, 2], "int32"),
     "kp": ("sbuf", [128, 16], "int32"),
-    "kk": ("sbuf", [128, TC], "int32"),
-    "kkf": ("sbuf", [128, TC], "float32"),
-    "mmod": ("sbuf", [128, 128], "float32"),
+    "kk": ("sbuf", [128, KW], "int32"),
+    "kkb": ("sbuf", [128, KW], "bfloat16"),
+    "dk": ("sbuf", [128, 128], "bfloat16"),
     "kidx": ("sbuf", [128, 1], "float32"),
     "nck": ("sbuf", [128, 16], "int32"),
-    "c16x": ("sbuf", [128, 97], "float32"),
+    "c16b": ("sbuf", [128, 97], "bfloat16"),
+    "v64": ("sbuf", [128, 16], "bfloat16"),
     "ones": ("sbuf", [128, 128], "bfloat16"),
     "zer": ("sbuf", [128, 16], "bfloat16"),
+    "c15": ("sbuf", [128, KW], "bfloat16"),
     "rm": ("sbuf", [128, 128], "bfloat16"),
     "wp": ("sbuf", [128, 128], "bfloat16"),
     "ck": ("sbuf", [128, 16], "bfloat16"),
     "cq1": ("sbuf", [128, 96], "bfloat16"),
-    "cq2": ("sbuf", [128, 96], "bfloat16"),
     "tri": ("sbuf", [128, 16], "bfloat16"),
+    "ntri": ("sbuf", [128, 16], "bfloat16"),
+    "tris": ("sbuf", [128, 16], "bfloat16"),
     "kpf": ("sbuf", [128, 16], "bfloat16"),
     "kneg": ("sbuf", [128, 16], "bfloat16"),
     "xinc": ("sbuf", [128, 16], "bfloat16"),
     "dst16": ("sbuf", [128, 16], "uint16"),
-    "nf": ("sbuf", [128, 1], "float32"),
-    "nb": ("sbuf", [128, 1], "bfloat16"),
     "gap": ("sbuf", [128, 1], "float32"),
     "offp": ("sbuf", [128, 1], "float32"),
     "offi": ("sbuf", [128, 1], "int32"),
@@ -49,30 +52,37 @@ SCRATCH = {
     "psd": ("psum", [128, 512], "float32"),
     "psf": ("psum", [128, 512], "float32"),
     "pso": ("psum", [128, 512], "float32"),
+    "psg": ("psum", [128, 512], "float32"),
 }
-SEMAPHORES = ["c0", "cv", "kld", "xld", "kown", "karr", "kload", "a1", "a2", "a3", "a4", "bready", "own", "arrived",
-              "b1", "b2", "b3", "b4", "b5", "b6", "b7", "b8", "b9", "b10", "b11", "st", "sent",
+SEMAPHORES = ["c0", "c1", "cv", "cw", "kld", "xld", "kown", "karr", "kload", "a1", "a2", "a3", "a4", "bready", "own",
+              "arrived", "b1", "b4", "b5", "b6", "b7", "b8", "b9", "b10", "b11", "st", "sent",
               "g0", "g1", "g2", "g3", "g4", "g5", "g6", "g7"]
+
+
+def _count(m):
+    return bin(m).count("1")
 
 
 def make_plan(cores, topo):
     load = {}
     plan = []
     for s, R in enumerate(cores):
-        mates = [c for c in range(NSIM) if c != R and topo.host(c) == topo.host(R) and topo.chip(c) == topo.chip(R)]
+        chipm = [c for c in range(NSIM) if c != R and topo.host(c) == topo.host(R) and topo.chip(c) == topo.chip(R)]
         others = [cores[(s + 1 + j) % len(cores)] for j in range(len(cores) - 1)]
         cross = [d for d in others if not topo.may_write(R, d)]
         same = [d for d in others if topo.may_write(R, d)]
-        owners = [c for c in mates if all(topo.may_write(c, d) for d in others)]
-        plain = [c for c in mates if c not in owners]
+        owners = [c for c in chipm if all(topo.may_write(c, d) for d in others)]
+        plain = [c for c in chipm if c not in owners]
         near, far = topo.die(R), 1 - topo.die(R)
-        H = ([c for c in owners if topo.die(c) == far][:2] + [c for c in owners if topo.die(c) == near][:2]
-             + [c for c in plain if topo.die(c) == far][:2])
+        on = [c for c in owners if topo.die(c) == near]
+        of = [c for c in owners if topo.die(c) == far]
+        pn = [c for c in plain if topo.die(c) == near]
+        pf = [c for c in plain if topo.die(c) == far]
+        H = [on[0], of[0], of[1], on[1], pf[0], pn[0]]
         cap = dict(zip(H, CAPS))
-        cap[R] = len(others) - sum(CAPS)
-        far_own = sum(cap[c] for c in H[0:2])
-        near_own = sum(cap[c] for c in H[2:4])
-        far_all = far_own + sum(cap[c] for c in H[4:6])
+        far_own = cap[of[0]] + cap[of[1]]
+        near_own = cap[on[0]] + cap[on[1]]
+        far_all = far_own + cap[pf[0]]
         fc = min(far_own, max(len(cross) - near_own, (len(cross) + 1) // 2))
 
         def lean(d):
@@ -81,32 +91,29 @@ def make_plan(cores, topo):
         ss = sorted(same, key=lean)
         cf, cn = cs[:fc], cs[fc:]
         sf, sn = ss[:far_all - fc], ss[far_all - fc:]
-        give = dict((c, []) for c in H + [R])
+        give = dict((c, []) for c in H)
 
         def deal(ds, cs_):
             for d in ds:
                 c = [c for c in cs_ if len(give[c]) < cap[c]][0]
                 give[c].append(d)
                 load[(d, topo.die(c))] = load.get((d, topo.die(c)), 0) + 1
-        deal(cf, H[0:2])
-        deal(cn, H[2:4])
-        deal(sf, H[4:6] + H[0:2])
-        deal(sn, [R] + H[2:4])
+        deal(cf, of[0:2])
+        deal(cn, on[0:2])
+        deal(sf, [pf[0]] + of[0:2])
+        deal(sn, [pn[0]] + on[0:2])
         plan.append({"R": R, "H": H, "give": give})
     return plan
 
 
-def _send(g, T, topo, core, groups, src, dst_of, rsem):
-    trs = []
-    for m, ds in groups:
-        ids = []
-        for d in ds:
-            rid, pid = topo.addr(d, core)
-            ids.append(DstId(rid=rid, pnc=pid))
-        trs.append(RemoteDMATransfer(dst_ids=ids, dma_engine_mask=m, remote_sem=rsem, srcs=[src],
-                                     dsts=[dst_of(d) for d in ds]))
-    g.remote_dma_fused(trs, local_sem=T.sem.sent)
-    return sum(bin(m).count("1") for m, ds in groups)
+def _send(g, T, topo, core, m, ds, src, dst, rsem):
+    ids = []
+    for d in ds:
+        rid, pid = topo.addr(d, core)
+        ids.append(DstId(rid=rid, pnc=pid))
+    g.remote_dma_fused([RemoteDMATransfer(dst_ids=ids, dma_engine_mask=m, remote_sem=rsem, srcs=[src],
+                                          dsts=[dst for d in ds])], local_sem=T.sem.sent)
+    return _count(m)
 
 
 def rank_program(g, core, T, topo):
@@ -122,32 +129,24 @@ def rank_program(g, core, T, topo):
     S = T.sem
     A = AluOpType
     P16 = slice(0, 16)
+    PK = slice(0, KP)
 
     ACT.dma_start(T.kp[P16, 0:16], T.keep[:]).then_inc(S.kld, 16)
+    SY.dma_start(T.kall[s], T.keep[:]).then_inc(S.kown, 16)
     SY.dma_start(T.xin[:, :], T.x[:]).then_inc(S.xld, 16)
-    ACT.dma_start(T.kall[s], T.keep[:]).then_inc(S.kown, 16)
 
-    g.iota(T.mmod[P16, :], [[0, 8], [1, 16]], 0, 0, allow_small_or_imprecise_dtypes=True).then_inc(S.c0, 1)
-    g.iota(T.kidx[P16, :], [[0, 1]], 0, 1, allow_small_or_imprecise_dtypes=True).then_inc(S.c0, 1)
+    g.iota(T.dk[P16, :], [[0, 8], [1, 16]], 0, -1, allow_small_or_imprecise_dtypes=True).then_inc(S.c0, 1)
     g.iota(T.nck[P16, :], [[16, 16]], -255, 1).then_inc(S.c0, 1)
-    g.iota(T.c16x[P16, :], [[16, 97]], 0, 0, allow_small_or_imprecise_dtypes=True).then_inc(S.c0, 1)
     V.memset(T.ones[P16, :], 1.0).then_inc(S.cv, 1)
     V.memset(T.zer[P16, :], 0.0).then_inc(S.cv, 1)
-    V.memset(T.land[:, W:W + 4], 0.0).then_inc(S.cv, 1)
-    V.wait_ge(S.c0, 4)
-    kx = T.kidx[P16, 0:1]
-    V.tensor_scalar(T.rm[P16, :], T.mmod[P16, :], kx, None, A.is_equal).then_inc(S.cv, 1)
-    V.tensor_scalar(T.wp[P16, :], T.mmod[P16, :], kx, -1.0, A.is_le, A.mult).then_inc(S.cv, 1)
+    V.wait_ge(S.c0, 2)
+    V.tensor_scalar(T.rm[P16, :], T.dk[P16, :], 0.0, None, A.is_equal).then_inc(S.cv, 1)
+    V.tensor_scalar(T.wp[P16, :], T.dk[P16, :], 0.0, -1.0, A.is_le, A.mult).then_inc(S.cv, 1)
     V.tensor_scalar(T.ck[P16, :], T.nck[P16, :], -1.0, None, A.mult).then_inc(S.cv, 1)
-    V.tensor_scalar(T.cq1[P16, :], T.c16x[P16, 0:96], 0.0, kx, A.mult, A.add).then_inc(S.cv, 1)
-    V.tensor_copy(T.cq2[P16, :], T.c16x[P16, 0:96]).then_inc(S.cv, 1)
-    V.tensor_scalar(T.tri[P16, :], T.mmod[P16, 0:16], kx, None, A.is_ge).then_inc(S.cv, 1)
-    NCV = 9
+    NCV = 5
     V.wait_ge(S.cv, NCV)
     PE.wait_ge(S.cv, NCV)
     PE.matmul(T.psd[:, 0:16], T.rm[P16, :], T.ck[P16, :], True, False).then_inc(S.a3, 1)
-    PE.matmul(T.psf[:, 0:96], T.rm[P16, :], T.cq1[P16, :], True, False).then_inc(S.b9, 1)
-    PE.matmul(T.psf[:, 0:96], T.rm[P16, :], T.cq2[P16, :], False, False).then_inc(S.b9, 1)
 
     V.wait_ge(S.kld, 16)
     V.tensor_copy(T.kpf[P16, :], T.kp[P16, :]).then_inc(S.a1, 1)
@@ -166,43 +165,60 @@ def rank_program(g, core, T, topo):
     V.tensor_copy(T.xs[:, 0:TC].indirect(T.dst16[:, 0:16]), T.xin[:, :]).then_inc(S.bready, 1)
 
     H, give = p["H"], p["give"]
-    lo_m = topo.mask(core, give[core][0])
-    hi_m = topo.mask(core, H[0]) & ~lo_m
-    groups = [(hi_m, H[0::2]), (lo_m, H[1::2] + give[core])]
+    fm = topo.mask(core, H[0])
     g.wait_ge(S.kown, 16)
-    sent = _send(g, T, topo, core, groups, T.kall[s], lambda d: T.kd[:] if d in H else T.kall[s], S.karr)
+    sent = _send(g, T, topo, core, fm, H, T.kall[s], T.kd[:], S.karr)
     g.wait_ge(S.bready, 1)
-    slot = T.land[:, CAP * s:CAP * (s + 1)]
-    sent += _send(g, T, topo, core, groups, T.xs[:, 0:CAP], lambda d: T.hb[:, :] if d in H else slot, S.arrived)
+    sent += _send(g, T, topo, core, fm, H, T.xs[:, 0:CAP], T.hb[:, :], S.arrived)
+    g.iota(T.kidx[P16, :], [[0, 1]], 0, 1, allow_small_or_imprecise_dtypes=True).then_inc(S.c1, 1)
+    g.iota(T.v64[PK, :], [[KP // N, 16]], KP // N - 1, -1, allow_small_or_imprecise_dtypes=True).then_inc(S.c1, 1)
+    g.iota(T.c16b[P16, :], [[16, 97]], 0, 0, allow_small_or_imprecise_dtypes=True).then_inc(S.c1, 1)
+    NC1 = 3
 
+    slot = T.land[:, CAP * s:CAP * (s + 1)]
     V.wait_ge(S.bready, 1)
     V.tensor_copy(slot, T.xs[:, 0:CAP]).then_inc(S.own, 1)
 
-    ne = bin(lo_m).count("1")
+    V.memset(T.land[:, W:W + 4], 0.0).then_inc(S.cw, 1)
+    V.memset(T.c15[P16, :], float(CAP) / (16 * KW)).then_inc(S.cw, 1)
+    V.wait_ge(S.c1, NC1)
+    kx = T.kidx[P16, 0:1]
+    V.tensor_scalar(T.tri[PK, :], T.v64[PK, :], 0.0, None, A.is_ge).then_inc(S.cw, 1)
+    V.tensor_scalar(T.ntri[PK, :], T.v64[PK, :], 0.0, -1.0, A.is_ge, A.mult).then_inc(S.cw, 1)
+    V.tensor_scalar(T.tris[PK, :], T.v64[PK, :], float(KP // N), None, A.is_ge).then_inc(S.cw, 1)
+    V.tensor_scalar(T.cq1[P16, :], T.c16b[P16, 0:96], 0.0, kx, A.mult, A.add).then_inc(S.cw, 1)
+    NCW = 6
+    V.wait_ge(S.cw, NCW)
+    PE.wait_ge(S.cw, NCW)
+    PE.wait_ge(S.c1, NC1)
+    PE.matmul(T.psg[P16, 0:KW], T.ones[P16, 0:16], T.c15[P16, :], True, False).then_inc(S.b4, 1)
+    PE.matmul(T.psf[:, 0:96], T.rm[P16, :], T.cq1[P16, :], True, False).then_inc(S.b9, 1)
+    PE.matmul(T.psf[:, 0:96], T.rm[P16, :], T.c16b[P16, 0:96], False, False).then_inc(S.b9, 1)
+
+    ne = _count(topo.mask(H[0], give[H[0]][0]))
     SY.wait_ge(S.kown, 16)
     SY.wait_ge(S.karr, ne * (N - 1))
-    SY.dma_start(T.kk[P16, :], T.kall[:]).then_inc(S.kload, 16)
+    SY.dma_start(T.kk[PK, :], T.kall[:]).then_inc(S.kload, 16)
     V.wait_ge(S.kload, 16)
-    V.tensor_copy(T.kkf[P16, :], T.kk[P16, :]).then_inc(S.b1, 1)
+    V.tensor_copy(T.kkb[PK, :], T.kk[PK, :]).then_inc(S.b1, 1)
+    PE.wait_ge(S.b1, 1)
+    PE.matmul(T.pso[P16, 0:KW], T.tri[PK, :], T.kkb[PK, :], True, True).then_inc(S.b4, 1)
+    PE.matmul(T.psg[P16, 0:KW], T.tris[PK, :], T.kkb[PK, :], False, False).then_inc(S.b4, 1)
+    PE.matmul(T.psg[P16, 0:KW], T.ntri[PK, :], T.kkb[PK, :], False, True).then_inc(S.b4, 1)
     V.wait_ge(S.b1, 1)
-    V.tensor_reduce(T.nf[P16, :], T.kkf[P16, :], AxisListType.X, A.add).then_inc(S.b2, 1)
-    V.wait_ge(S.b2, 1)
-    V.tensor_copy(T.nb[P16, :], T.nf[P16, :]).then_inc(S.b3, 1)
-    V.tensor_scalar(T.gap[P16, :], T.nf[P16, :], -1.0, float(CAP), A.mult, A.add).then_inc(S.b3, 1)
-    PE.wait_ge(S.b3, 2)
-    PE.matmul(T.pso[P16, 0:1], T.tri[P16, :], T.nb[P16, :], True, True).then_inc(S.b4, 1)
-    V.wait_ge(S.b3, 2)
-    V.wait_ge(S.b4, 1)
-    V.tensor_copy(T.offp[P16, :], T.pso[P16, 0:1]).then_inc(S.b5, 1)
-    V.tensor_copy(T.offi[P16, :], T.pso[P16, 0:1]).then_inc(S.b5, 1)
+    V.wait_ge(S.b4, 4)
+    V.tensor_reduce(T.offp[P16, :], T.pso[P16, 0:KW], AxisListType.X, A.add).then_inc(S.b5, 1)
+    V.tensor_reduce(T.gap[P16, :], T.psg[P16, 0:KW], AxisListType.X, A.add).then_inc(S.b5, 1)
     V.wait_ge(S.b5, 2)
-    V.tensor_scalar(T.rhx[P16, :], T.c16x[P16, :], T.offp[P16, 0:1], None, A.is_gt).then_inc(S.b6, 1)
+    V.tensor_copy(T.offi[P16, :], T.offp[P16, :]).then_inc(S.b11, 1)
+    V.tensor_scalar(T.rhx[P16, :], T.c16b[P16, :], T.offp[P16, 0:1], None, A.is_gt).then_inc(S.b6, 1)
+    V.wait_ge(S.b11, 1)
     V.tensor_scalar(T.loi[P16, :], T.offi[P16, :], 15, None, A.bitwise_and).then_inc(S.b7, 1)
     V.wait_ge(S.b7, 1)
-    V.tensor_copy(T.lo[P16, :], T.loi[P16, :]).then_inc(S.b8, 1)
+    V.tensor_scalar(T.lo[P16, :], T.loi[P16, :], kx, None, A.subtract).then_inc(S.b8, 1)
     V.wait_ge(S.b8, 1)
-    V.tensor_scalar(T.lta[P16, :], T.mmod[P16, :], T.lo[P16, 0:1], T.gap[P16, 0:1], A.is_lt, A.mult).then_inc(S.b6, 1)
-    V.tensor_scalar(T.ltb[P16, :], T.mmod[P16, :], T.lo[P16, 0:1], T.gap[P16, 0:1], A.is_ge, A.mult).then_inc(S.b6, 1)
+    V.tensor_scalar(T.lta[P16, :], T.dk[P16, :], T.lo[P16, 0:1], T.gap[P16, 0:1], A.is_lt, A.mult).then_inc(S.b6, 1)
+    V.tensor_scalar(T.ltb[P16, :], T.dk[P16, :], T.lo[P16, 0:1], T.gap[P16, 0:1], A.is_ge, A.mult).then_inc(S.b6, 1)
     PE.wait_ge(S.b6, 3)
     PE.matmul(T.psf[:, 0:96], T.lta[P16, :], T.rhx[P16, 0:96], False, False).then_inc(S.b9, 1)
     PE.matmul(T.psf[:, 0:96], T.ltb[P16, :], T.rhx[P16, 1:97], False, True).then_inc(S.b9, 1)
@@ -212,6 +228,7 @@ def rank_program(g, core, T, topo):
 
     win = T.land[:, 0:W + 1]
     for q in (V, ACT):
+        q.wait_ge(S.cw, NCW)
         q.wait_ge(S.b10, 1)
         q.wait_ge(S.own, 1)
         q.wait_ge(S.arrived, ne * (N - 1))
@@ -239,12 +256,9 @@ def helper_program(g, core, T, topo, s, p):
     S = T.sem
     ds = p["give"][core]
     m = topo.mask(core, ds[0])
-    R = p["R"]
-    lo_m = topo.mask(R, p["give"][R][0])
-    hi_m = topo.mask(R, core) & ~lo_m
-    got = bin(hi_m if p["H"].index(core) % 2 == 0 else lo_m).count("1")
+    got = _count(topo.mask(p["R"], core))
     g.wait_ge(S.karr, got)
-    sent = _send(g, T, topo, core, [(m, ds)], T.kd[:], lambda d: T.kall[s], S.karr)
+    sent = _send(g, T, topo, core, m, ds, T.kd[:], T.kall[s], S.karr)
     g.wait_ge(S.arrived, got)
-    sent += _send(g, T, topo, core, [(m, ds)], T.hb[:, :], lambda d: T.land[:, CAP * s:CAP * (s + 1)], S.arrived)
+    sent += _send(g, T, topo, core, m, ds, T.hb[:, :], T.land[:, CAP * s:CAP * (s + 1)], S.arrived)
     g.wait_ge(S.sent, sent)

from concourse.bass import DstId, RemoteDMATransfer
from concourse.mybir import AluOpType, AxisListType, ActivationFunctionType

NSIM = 256
N, TC, CAP = 16, 256, 96
W = N * CAP
CAPS = (4, 3, 3, 2, 2, 1)
VCH = ((0, 24), (24, 48))
ACH = ((48, 72), (72, 96))
KP = 64
KW = N * TC // KP

SCRATCH = {
    "xin": ("sbuf", [128, TC], "float32"),
    "xs": ("sbuf", [128, TC], "float32"),
    "hb": ("sbuf", [128, CAP], "float32"),
    "land": ("sbuf", [128, W + 4], "float32"),
    "yo": ("sbuf", [128, W], "float32"),
    "kd": ("dram", [128, 2], "int32"),
    "kall": ("dram", [N, 128, 2], "int32"),
    "kp": ("sbuf", [128, 16], "int32"),
    "kk": ("sbuf", [128, KW], "int32"),
    "kkb": ("sbuf", [128, KW], "bfloat16"),
    "dk": ("sbuf", [128, 128], "bfloat16"),
    "kidx": ("sbuf", [128, 1], "float32"),
    "nck": ("sbuf", [128, 16], "int32"),
    "c16b": ("sbuf", [128, 97], "bfloat16"),
    "v64": ("sbuf", [128, 16], "bfloat16"),
    "ones": ("sbuf", [128, 128], "bfloat16"),
    "zer": ("sbuf", [128, 16], "bfloat16"),
    "c15": ("sbuf", [128, KW], "bfloat16"),
    "rm": ("sbuf", [128, 128], "bfloat16"),
    "wp": ("sbuf", [128, 128], "bfloat16"),
    "ck": ("sbuf", [128, 16], "bfloat16"),
    "cq1": ("sbuf", [128, 96], "bfloat16"),
    "tri": ("sbuf", [128, 16], "bfloat16"),
    "ntri": ("sbuf", [128, 16], "bfloat16"),
    "tris": ("sbuf", [128, 16], "bfloat16"),
    "kpf": ("sbuf", [128, 16], "bfloat16"),
    "kneg": ("sbuf", [128, 16], "bfloat16"),
    "xinc": ("sbuf", [128, 16], "bfloat16"),
    "dst16": ("sbuf", [128, 16], "uint16"),
    "gap": ("sbuf", [128, 1], "float32"),
    "offp": ("sbuf", [128, 1], "float32"),
    "offi": ("sbuf", [128, 1], "int32"),
    "loi": ("sbuf", [128, 1], "int32"),
    "lo": ("sbuf", [128, 1], "float32"),
    "rhx": ("sbuf", [128, 97], "bfloat16"),
    "lta": ("sbuf", [128, 128], "bfloat16"),
    "ltb": ("sbuf", [128, 128], "bfloat16"),
    "offs": ("sbuf", [128, 96], "uint16"),
    "psd": ("psum", [128, 512], "float32"),
    "psf": ("psum", [128, 512], "float32"),
    "pso": ("psum", [128, 512], "float32"),
    "psg": ("psum", [128, 512], "float32"),
}
SEMAPHORES = ["c0", "c1", "cv", "cw", "kld", "xld", "kown", "karr", "kload", "a1", "a2", "a3", "a4", "bready", "own",
              "arrived", "b1", "b4", "b5", "b6", "b7", "b8", "b9", "b10", "b11", "st", "sent",
              "g0", "g1", "g2", "g3", "g4", "g5", "g6", "g7"]


def _count(m):
    return bin(m).count("1")


def make_plan(cores, topo):
    load = {}
    plan = []
    for s, R in enumerate(cores):
        chipm = [c for c in range(NSIM) if c != R and topo.host(c) == topo.host(R) and topo.chip(c) == topo.chip(R)]
        others = [cores[(s + 1 + j) % len(cores)] for j in range(len(cores) - 1)]
        cross = [d for d in others if not topo.may_write(R, d)]
        same = [d for d in others if topo.may_write(R, d)]
        owners = [c for c in chipm if all(topo.may_write(c, d) for d in others)]
        plain = [c for c in chipm if c not in owners]
        near, far = topo.die(R), 1 - topo.die(R)
        on = [c for c in owners if topo.die(c) == near]
        of = [c for c in owners if topo.die(c) == far]
        pn = [c for c in plain if topo.die(c) == near]
        pf = [c for c in plain if topo.die(c) == far]
        H = [on[0], of[0], of[1], on[1], pf[0], pn[0]]
        cap = dict(zip(H, CAPS))
        far_own = cap[of[0]] + cap[of[1]]
        near_own = cap[on[0]] + cap[on[1]]
        far_all = far_own + cap[pf[0]]
        fc = min(far_own, max(len(cross) - near_own, (len(cross) + 1) // 2))

        def lean(d):
            return load.get((d, far), 0) - load.get((d, near), 0)
        cs = sorted(cross, key=lean)
        ss = sorted(same, key=lean)
        cf, cn = cs[:fc], cs[fc:]
        sf, sn = ss[:far_all - fc], ss[far_all - fc:]
        give = dict((c, []) for c in H)

        def deal(ds, cs_):
            for d in ds:
                c = [c for c in cs_ if len(give[c]) < cap[c]][0]
                give[c].append(d)
                load[(d, topo.die(c))] = load.get((d, topo.die(c)), 0) + 1
        deal(cf, of[0:2])
        deal(cn, on[0:2])
        deal(sf, [pf[0]] + of[0:2])
        deal(sn, [pn[0]] + on[0:2])
        plan.append({"R": R, "H": H, "give": give})
    return plan


def _send(g, T, topo, core, m, ds, src, dst, rsem):
    ids = []
    for d in ds:
        rid, pid = topo.addr(d, core)
        ids.append(DstId(rid=rid, pnc=pid))
    g.remote_dma_fused([RemoteDMATransfer(dst_ids=ids, dma_engine_mask=m, remote_sem=rsem, srcs=[src],
                                          dsts=[dst for d in ds])], local_sem=T.sem.sent)
    return _count(m)


def rank_program(g, core, T, topo):
    plan = make_plan(list(T.cores), topo)
    rank = T.rank_of(core)
    if rank is None:
        for s, p in enumerate(plan):
            if core in p["H"] and p["give"][core]:
                helper_program(g, core, T, topo, s, p)
        return
    s, p = rank, plan[rank]
    V, PE, ACT, SY = g.vector, g.tensor, g.scalar, g.sync
    S = T.sem
    A = AluOpType
    P16 = slice(0, 16)
    PK = slice(0, KP)

    ACT.dma_start(T.kp[P16, 0:16], T.keep[:]).then_inc(S.kld, 16)
    SY.dma_start(T.kall[s], T.keep[:]).then_inc(S.kown, 16)
    SY.dma_start(T.xin[:, :], T.x[:]).then_inc(S.xld, 16)

    g.iota(T.dk[P16, :], [[0, 8], [1, 16]], 0, -1, allow_small_or_imprecise_dtypes=True).then_inc(S.c0, 1)
    g.iota(T.nck[P16, :], [[16, 16]], -255, 1).then_inc(S.c0, 1)
    V.memset(T.ones[P16, :], 1.0).then_inc(S.cv, 1)
    V.memset(T.zer[P16, :], 0.0).then_inc(S.cv, 1)
    V.wait_ge(S.c0, 2)
    V.tensor_scalar(T.rm[P16, :], T.dk[P16, :], 0.0, None, A.is_equal).then_inc(S.cv, 1)
    V.tensor_scalar(T.wp[P16, :], T.dk[P16, :], 0.0, -1.0, A.is_le, A.mult).then_inc(S.cv, 1)
    V.tensor_scalar(T.ck[P16, :], T.nck[P16, :], -1.0, None, A.mult).then_inc(S.cv, 1)
    NCV = 5
    V.wait_ge(S.cv, NCV)
    PE.wait_ge(S.cv, NCV)
    PE.matmul(T.psd[:, 0:16], T.rm[P16, :], T.ck[P16, :], True, False).then_inc(S.a3, 1)

    V.wait_ge(S.kld, 16)
    V.tensor_copy(T.kpf[P16, :], T.kp[P16, :]).then_inc(S.a1, 1)
    V.tensor_tensor(T.kneg[P16, :], T.kp[P16, :], T.nck[P16, :], A.mult).then_inc(S.a1, 1)
    V.wait_ge(S.a1, 2)
    V.tensor_tensor_scan(T.xinc[P16, :], T.kpf[P16, :], T.zer[P16, :], 0.0, A.add, A.add).then_inc(S.a2, 1)
    PE.wait_ge(S.a1, 2)
    PE.matmul(T.psd[:, 0:16], T.wp[P16, :], T.kpf[P16, :], False, False).then_inc(S.a3, 1)
    PE.matmul(T.psd[:, 0:16], T.rm[P16, :], T.kneg[P16, :], False, False).then_inc(S.a3, 1)
    PE.wait_ge(S.a2, 1)
    PE.matmul(T.psd[:, 0:16], T.ones[P16, :], T.xinc[P16, :], False, True).then_inc(S.a3, 1)
    V.wait_ge(S.a3, 4)
    V.tensor_copy(T.dst16[:, :], T.psd[:, 0:16]).then_inc(S.a4, 1)
    V.wait_ge(S.a4, 1)
    V.wait_ge(S.xld, 16)
    V.tensor_copy(T.xs[:, 0:TC].indirect(T.dst16[:, 0:16]), T.xin[:, :]).then_inc(S.bready, 1)

    H, give = p["H"], p["give"]
    fm = topo.mask(core, H[0])
    g.wait_ge(S.kown, 16)
    sent = _send(g, T, topo, core, fm, H, T.kall[s], T.kd[:], S.karr)
    g.wait_ge(S.bready, 1)
    sent += _send(g, T, topo, core, fm, H, T.xs[:, 0:CAP], T.hb[:, :], S.arrived)
    g.iota(T.kidx[P16, :], [[0, 1]], 0, 1, allow_small_or_imprecise_dtypes=True).then_inc(S.c1, 1)
    g.iota(T.v64[PK, :], [[KP // N, 16]], KP // N - 1, -1, allow_small_or_imprecise_dtypes=True).then_inc(S.c1, 1)
    g.iota(T.c16b[P16, :], [[16, 97]], 0, 0, allow_small_or_imprecise_dtypes=True).then_inc(S.c1, 1)
    NC1 = 3

    slot = T.land[:, CAP * s:CAP * (s + 1)]
    V.wait_ge(S.bready, 1)
    V.tensor_copy(slot, T.xs[:, 0:CAP]).then_inc(S.own, 1)

    V.memset(T.land[:, W:W + 4], 0.0).then_inc(S.cw, 1)
    V.memset(T.c15[P16, :], float(CAP) / (16 * KW)).then_inc(S.cw, 1)
    V.wait_ge(S.c1, NC1)
    kx = T.kidx[P16, 0:1]
    V.tensor_scalar(T.tri[PK, :], T.v64[PK, :], 0.0, None, A.is_ge).then_inc(S.cw, 1)
    V.tensor_scalar(T.ntri[PK, :], T.v64[PK, :], 0.0, -1.0, A.is_ge, A.mult).then_inc(S.cw, 1)
    V.tensor_scalar(T.tris[PK, :], T.v64[PK, :], float(KP // N), None, A.is_ge).then_inc(S.cw, 1)
    V.tensor_scalar(T.cq1[P16, :], T.c16b[P16, 0:96], 0.0, kx, A.mult, A.add).then_inc(S.cw, 1)
    NCW = 6
    V.wait_ge(S.cw, NCW)
    PE.wait_ge(S.cw, NCW)
    PE.wait_ge(S.c1, NC1)
    PE.matmul(T.psg[P16, 0:KW], T.ones[P16, 0:16], T.c15[P16, :], True, False).then_inc(S.b4, 1)
    PE.matmul(T.psf[:, 0:96], T.rm[P16, :], T.cq1[P16, :], True, False).then_inc(S.b9, 1)
    PE.matmul(T.psf[:, 0:96], T.rm[P16, :], T.c16b[P16, 0:96], False, False).then_inc(S.b9, 1)

    ne = _count(topo.mask(H[0], give[H[0]][0]))
    SY.wait_ge(S.kown, 16)
    SY.wait_ge(S.karr, ne * (N - 1))
    SY.dma_start(T.kk[PK, :], T.kall[:]).then_inc(S.kload, 16)
    V.wait_ge(S.kload, 16)
    V.tensor_copy(T.kkb[PK, :], T.kk[PK, :]).then_inc(S.b1, 1)
    PE.wait_ge(S.b1, 1)
    PE.matmul(T.pso[P16, 0:KW], T.tri[PK, :], T.kkb[PK, :], True, True).then_inc(S.b4, 1)
    PE.matmul(T.psg[P16, 0:KW], T.tris[PK, :], T.kkb[PK, :], False, False).then_inc(S.b4, 1)
    PE.matmul(T.psg[P16, 0:KW], T.ntri[PK, :], T.kkb[PK, :], False, True).then_inc(S.b4, 1)
    V.wait_ge(S.b1, 1)
    V.wait_ge(S.b4, 4)
    V.tensor_reduce(T.offp[P16, :], T.pso[P16, 0:KW], AxisListType.X, A.add).then_inc(S.b5, 1)
    V.tensor_reduce(T.gap[P16, :], T.psg[P16, 0:KW], AxisListType.X, A.add).then_inc(S.b5, 1)
    V.wait_ge(S.b5, 2)
    V.tensor_copy(T.offi[P16, :], T.offp[P16, :]).then_inc(S.b11, 1)
    V.tensor_scalar(T.rhx[P16, :], T.c16b[P16, :], T.offp[P16, 0:1], None, A.is_gt).then_inc(S.b6, 1)
    V.wait_ge(S.b11, 1)
    V.tensor_scalar(T.loi[P16, :], T.offi[P16, :], 15, None, A.bitwise_and).then_inc(S.b7, 1)
    V.wait_ge(S.b7, 1)
    V.tensor_scalar(T.lo[P16, :], T.loi[P16, :], kx, None, A.subtract).then_inc(S.b8, 1)
    V.wait_ge(S.b8, 1)
    V.tensor_scalar(T.lta[P16, :], T.dk[P16, :], T.lo[P16, 0:1], T.gap[P16, 0:1], A.is_lt, A.mult).then_inc(S.b6, 1)
    V.tensor_scalar(T.ltb[P16, :], T.dk[P16, :], T.lo[P16, 0:1], T.gap[P16, 0:1], A.is_ge, A.mult).then_inc(S.b6, 1)
    PE.wait_ge(S.b6, 3)
    PE.matmul(T.psf[:, 0:96], T.lta[P16, :], T.rhx[P16, 0:96], False, False).then_inc(S.b9, 1)
    PE.matmul(T.psf[:, 0:96], T.ltb[P16, :], T.rhx[P16, 1:97], False, True).then_inc(S.b9, 1)
    V.wait_ge(S.b6, 3)
    V.wait_ge(S.b9, 4)
    V.tensor_scalar(T.offs[:, :], T.psf[:, 0:96], float(W), None, A.min).then_inc(S.b10, 1)

    win = T.land[:, 0:W + 1]
    for q in (V, ACT):
        q.wait_ge(S.cw, NCW)
        q.wait_ge(S.b10, 1)
        q.wait_ge(S.own, 1)
        q.wait_ge(S.arrived, ne * (N - 1))
    order = []
    for j in range(max(len(VCH), len(ACH))):
        if j < len(VCH):
            a, b = VCH[j]
            sem = S["g%d" % (2 * j)]
            V.tensor_copy(T.yo[:, 16 * a:16 * b], win.indirect(T.offs[:, a:b])).then_inc(sem, 1)
            order.append((sem, a, b))
        if j < len(ACH):
            a, b = ACH[j]
            sem = S["g%d" % (2 * j + 1)]
            ACT.activation(T.yo[:, 16 * a:16 * b], win.indirect(T.offs[:, a:b]), ActivationFunctionType.Identity,
                           bias=-0.0).then_inc(sem, 1)
            order.append((sem, a, b))
    for sem, a, b in order:
        SY.wait_ge(sem, 1)
        SY.dma_start(T.y[:, 16 * a:16 * b], T.yo[:, 16 * a:16 * b]).then_inc(S.st, 16)
    SY.wait_ge(S.st, 16 * len(order))
    g.wait_ge(S.sent, sent)


def helper_program(g, core, T, topo, s, p):
    S = T.sem
    ds = p["give"][core]
    m = topo.mask(core, ds[0])
    got = _count(topo.mask(p["R"], core))
    g.wait_ge(S.karr, got)
    sent = _send(g, T, topo, core, m, ds, T.kd[:], T.kall[s], S.karr)
    g.wait_ge(S.arrived, got)
    sent += _send(g, T, topo, core, m, ds, T.hb[:, :], T.land[:, CAP * s:CAP * (s + 1)], S.arrived)
    g.wait_ge(S.sent, sent)
